import numpy as np
import ml_dtypes


def mxq(x, axis, fmt="e4m3"):
    dtype, down = {"e4m3": (ml_dtypes.float8_e4m3fn, 7), "e5m2": (ml_dtypes.float8_e5m2, 14)}[fmt]
    v = np.moveaxis(np.asarray(x, np.float32).astype(ml_dtypes.bfloat16).astype(np.float64), axis, -1)
    blocks = v.reshape(v.shape[:-1] + (-1, 32))
    amax = np.abs(blocks).max(-1, keepdims=True)
    byte = np.maximum(np.where(amax > 0, np.frexp(amax)[1] - 1 + 127, 0) - down, 1)
    scale = np.exp2(byte - 127.0)
    codes = (blocks / scale).astype(np.float32).astype(dtype).astype(np.float64)
    return np.moveaxis((codes * scale).reshape(v.shape), -1, axis)


WIDE = False


def mx_kscale(k):
    if not WIDE:
        return np.ones(k)
    levels = np.array([30, -30])
    if k % 512:
        return np.exp2(np.random.permutation(np.resize(levels, k // 32))).repeat(32)
    a = np.empty((k // 512, 16))
    for p in range(k // 512):
        a[p, :8] = np.random.permutation(np.resize(levels, 8))
        for g in range(8):
            far = levels[np.abs(levels - a[p, g]) >= 10]
            a[p, g + 8] = far[np.random.randint(len(far))]
    return np.exp2(a.ravel()).repeat(32)


def f64(x):
    return np.asarray(x).astype(np.float64)


def striped(idx):
    return np.tile(idx.reshape(-1, 16).T, (8, 1)).astype(np.uint16)


def unstriped(offs):
    return offs[:16].T.reshape(-1).astype(np.int64)


def relu(v):
    return np.maximum(v, 0.0)


def d_relu(v):
    return (v > 0).astype(np.float64)


K, T, E, C, H, N = 128, 2048, 4, 512, 512, 1024


def by_expert(wq, xq):
    return np.concatenate([wq[e].T @ xq[:, e * C:(e + 1) * C] for e in range(E)], axis=1)


def setup_inputs():
    n = np.random.standard_normal
    s = mx_kscale(N)[:, None]
    u = mx_kscale(H)
    return {
        "dyT": (n((N, T)) * s).astype(np.float32),
        "a1": n((H, E * C)).astype(np.float32),
        "a3": n((H, E * C)).astype(np.float32),
        "w2": (n((E, N, H)) / np.sqrt(N) / s[None] * u[None, None, :]).astype(np.float32),
        "w1": (n((E, H, K)) / np.sqrt(H) / u[None, :, None]).astype(np.float32),
        "w3": (n((E, H, K)) / np.sqrt(H) / u[None, :, None]).astype(np.float32),
        "gate": np.tile(np.random.uniform(0.2, 1.0, E * C), (N, 1)).astype(np.float32),
        "offs": striped(np.random.permutation(T)[:E * C]),
    }


def reference(dyT, a1, a3, w2, w1, w3, gate, offs):
    idx = unstriped(offs)
    gq = mxq(f64(gate) * f64(dyT)[:, idx], 0, "e5m2")
    dh = by_expert(mxq(f64(w2), 1, "e4m3"), gq)
    da1 = dh * f64(a3) * d_relu(f64(a1))
    da3 = dh * relu(f64(a1))
    dx = by_expert(mxq(f64(w1), 1, "e4m3"), mxq(da1, 0, "e5m2")) + by_expert(mxq(f64(w3), 1, "e4m3"), mxq(da3, 0, "e5m2"))
    out = np.zeros((K, T))
    out[:, idx] = dx
    return out

@@ -1,0 +1,231 @@
+from contextlib import ExitStack
+
+import concourse.mybir as mybir
+
+E, C, T, K, H, N = 4, 512, 2048, 128, 512, 1024
+P = 128
+PACK = 4
+PASSES = N // (P * PACK)
+PAIR = 2 * C
+
+F32 = mybir.dt.float32
+BF16 = mybir.dt.bfloat16
+U32 = mybir.dt.uint32
+U16 = mybir.dt.uint16
+U8 = mybir.dt.uint8
+E4M3X4 = mybir.dt.float8_e4m3fn_x4
+E5M2X4 = mybir.dt.float8_e5m2_x4
+MULT = mybir.AluOpType.mult
+RELU = mybir.ActivationFunctionType.Relu
+IS_GT = mybir.AluOpType.is_gt
+
+FLOPS = 2 * N * H * E * C + 2 * 2 * H * K * E * C
+BYTES = 4 * (N * T + 2 * H * E * C + E * N * H + 2 * E * H * K + E * C + K * T) + 2 * P * (E * C // 16)
+
+
+def tile_moe_bdx_glu_relu_kernel(tc, dyT, a1, a3, w2, w1, w3, gate, offs, out):
+    nc = tc.nc
+
+    dy_rows = dyT.rearrange("(c p t) w -> c t p w", c=PASSES, t=PACK)
+    w2_rows = w2.rearrange("e (c p j) i -> e c p j i", c=PASSES, j=PACK)
+    a1_rows = a1.rearrange("(p t) (e s) -> e p t s", t=PACK, e=E)
+    a3_rows = a3.rearrange("(p t) (e s) -> e p t s", t=PACK, e=E)
+
+    with ExitStack() as ctx:
+        held = ctx.enter_context(tc.tile_pool(name="held", bufs=1))
+        raw = ctx.enter_context(tc.tile_pool(name="raw", bufs=11))
+        gpool = ctx.enter_context(tc.tile_pool(name="gpool", bufs=2))
+        work = ctx.enter_context(tc.tile_pool(name="work", bufs=2))
+        codes = ctx.enter_context(tc.tile_pool(name="codes", bufs=6))
+        psum = ctx.enter_context(tc.psum_pool(name="psum", bufs=1))
+
+        def load(src, shape):
+            big = raw.tile(shape, F32, tag="big", align_bytes=64, name="big")
+            nc.sync.dma_start(big[:], src)
+            return big
+
+        def quantize(src, tag, dtype, bufs):
+            words = codes.tile([P, C], U32, tag=tag + "_w", bufs=bufs, align_bytes=64, name=tag + "_w")
+            scales = codes.tile([P, C], U8, tag=tag + "_s", bufs=bufs, align_bytes=64, name=tag + "_s")
+            nc.vector.quantize_mx(out=words[:].bitcast(dtype), scales=scales[:], in_=src[:])
+            return words, scales
+
+        offsets = held.tile([P, E * C // 16], U16, name="offsets")
+        nc.sync.dma_start(offsets[:], offs)
+        dy = {}
+        gates = {}
+        for c in range(PASSES):
+            for t in range(PACK):
+                dy[c, t] = load(dy_rows[c, t], [P, T])
+                if c == 0 and t == 0:
+                    g0 = held.tile([P, PAIR], F32, name="g0")
+                    nc.sync.dma_start(g0[:], gate[0:P, 0:PAIR])
+                    gates[0] = g0
+        g1 = held.tile([P, PAIR], F32, name="g1")
+        nc.sync.dma_start(g1[:], gate[0:P, PAIR : 2 * PAIR])
+        gates[1] = g1
+        w2_raw = {}
+        w2_raw[0, 0] = load(w2_rows[0, 0], [P, PACK, H])
+        w2_raw[0, 1] = load(w2_rows[0, 1], [P, PACK, H])
+        w1_raw = load(w1.rearrange("e (p j) k -> p e j k", j=PACK), [P, E, PACK, K])
+
+        result = held.tile([P, T], F32, name="result")
+
+        g_q = {}
+        w2_q = {}
+
+        def gather(pair, c, t, planes):
+            nc.vector.tensor_tensor(
+                planes[:, t, :],
+                dy[c, t][:].indirect(offsets[:, pair * PAIR // 16 : (pair + 1) * PAIR // 16]),
+                gates[pair][:],
+                MULT,
+            )
+
+        def prepare_g(pair, c, planes):
+            for h in range(2):
+                e = 2 * pair + h
+                gb = work.tile([P, PACK * C], BF16, tag="gb", bufs=3, align_bytes=64, name="gb")
+                nc.scalar.copy(
+                    out=gb[:].rearrange("p (s i t) -> p s t i", i=4, t=PACK),
+                    in_=planes[:, :, h * C : (h + 1) * C].rearrange("p t (s i) -> p s t i", i=4),
+                )
+                g_q[e, c] = quantize(gb, "g", E5M2X4, 6)
+
+        def prepare_w2(e):
+            for c in range(PASSES):
+                wb = work.tile([P, PACK * H], BF16, tag="wb", bufs=2, align_bytes=64, name="wb")
+                nc.scalar.copy(
+                    out=wb[:].rearrange("p (t m j) -> p m j t", t=PACK, j=PACK),
+                    in_=w2_raw[e, c][:].rearrange("p j (m t) -> p m j t", t=PACK),
+                )
+                w2_q[e, c] = quantize(wb, "w2", E4M3X4, 5)
+
+        def prepare_w13(src, tag):
+            wb = work.tile([P, PACK * H], BF16, tag="wb", bufs=2, align_bytes=64, name="wb")
+            nc.scalar.copy(
+                out=wb[:].rearrange("p (e k j) -> p e k j", e=E, j=PACK),
+                in_=src[:].rearrange("p e j k -> p e k j"),
+            )
+            return quantize(wb, tag, E4M3X4, 1)
+
+        def first_product(e):
+            dh = work.tile([P, PACK, C], F32, tag="dh", bufs=2, align_bytes=64, name="dh")
+            for t in range(PACK):
+                bank = psum.tile([P, C], F32, tag="bank", bufs=6, name="bank")
+                for c in range(PASSES):
+                    nc.tensor.matmul_mx(
+                        out=bank[:],
+                        lhsT=w2_q[e, c][0][:, t * P : (t + 1) * P].bitcast(E4M3X4),
+                        lhsT_scale=w2_q[e, c][1][:, t * P : (t + 1) * P],
+                        rhs=g_q[e, c][0][:].bitcast(E5M2X4),
+                        rhs_scale=g_q[e, c][1][:],
+                        start=(c == 0),
+                        stop=(c == PASSES - 1),
+                    )
+                nc.scalar.copy(out=dh[:, t, :], in_=bank[:])
+            return dh
+
+        a1_raw = {}
+        a3_raw = {}
+
+        def mask(e):
+            nc.scalar.activation(a1_raw[e][:], a1_raw[e][:], RELU)
+            nc.vector.scalar_tensor_tensor(a3_raw[e][:], a1_raw[e][:], 0.0, a3_raw[e][:], op0=IS_GT, op1=MULT)
+
+        def walk_in(x):
+            return x[:].rearrange("p t (s i) -> p s t i", i=4)
+
+        def derivative(e, dh):
+            d1 = work.tile([P, PACK * C], BF16, tag="da", bufs=3, align_bytes=64, name="d1")
+            d3 = work.tile([P, PACK * C], BF16, tag="da", bufs=3, align_bytes=64, name="d3")
+            nc.vector.tensor_tensor(
+                d1[:].rearrange("p (s i t) -> p s t i", i=4, t=PACK), walk_in(a3_raw[e]), walk_in(dh), MULT
+            )
+            nc.vector.tensor_tensor(
+                d3[:].rearrange("p (s i t) -> p s t i", i=4, t=PACK), walk_in(a1_raw[e]), walk_in(dh), MULT
+            )
+            return quantize(d1, "da", E5M2X4, 4), quantize(d3, "da", E5M2X4, 4)
+
+        def second_product(e, da):
+            bank = psum.tile([P, C], F32, tag="dx", bufs=2, name="dxbank")
+            for n, (wq, dq) in enumerate(zip((w1_q, w3_q), da)):
+                nc.tensor.matmul_mx(
+                    out=bank[:],
+                    lhsT=wq[0][:, e * K : (e + 1) * K].bitcast(E4M3X4),
+                    lhsT_scale=wq[1][:, e * K : (e + 1) * K],
+                    rhs=dq[0][:].bitcast(E5M2X4),
+                    rhs_scale=dq[1][:],
+                    start=(n == 0),
+                    stop=(n == 1),
+                )
+            dx = work.tile([P, C], F32, tag="dx", bufs=2, align_bytes=64, name="dx")
+            nc.scalar.copy(out=dx[:], in_=bank[:])
+            return dx
+
+        def scatter(e, dx):
+            nc.vector.tensor_copy(result[:].indirect(offsets[:, e * C // 16 : (e + 1) * C // 16]), dx[:])
+
+        for c in range(PASSES):
+            planes = gpool.tile([P, PACK, PAIR], F32, tag="planes", align_bytes=64, name="planes")
+            for t in range(PACK):
+                gather(0, c, t, planes)
+            prepare_g(0, c, planes)
+        prepare_w2(0)
+        w1_q = prepare_w13(w1_raw, "w1")
+
+        planes = gpool.tile([P, PACK, PAIR], F32, tag="planes", align_bytes=64, name="planes")
+        gather(1, 0, 0, planes)
+        w3_raw = load(w3.rearrange("e (p j) k -> p e j k", j=PACK), [P, E, PACK, K])
+        gather(1, 0, 1, planes)
+        a1_raw[0] = load(a1_rows[0], [P, PACK, C])
+        gather(1, 0, 2, planes)
+        a3_raw[0] = load(a3_rows[0], [P, PACK, C])
+        gather(1, 0, 3, planes)
+        w2_raw[1, 0] = load(w2_rows[1, 0], [P, PACK, H])
+        w3_q = prepare_w13(w3_raw, "w3")
+        dh = {}
+        dh[0] = first_product(0)
+        prepare_g(1, 0, planes)
+        planes = gpool.tile([P, PACK, PAIR], F32, tag="planes", align_bytes=64, name="planes")
+        gather(1, 1, 0, planes)
+        w2_raw[1, 1] = load(w2_rows[1, 1], [P, PACK, H])
+        gather(1, 1, 1, planes)
+        a1_raw[1] = load(a1_rows[1], [P, PACK, C])
+        gather(1, 1, 2, planes)
+        a3_raw[1] = load(a3_rows[1], [P, PACK, C])
+        gather(1, 1, 3, planes)
+        w2_raw[2, 0] = load(w2_rows[2, 0], [P, PACK, H])
+        w2_raw[2, 1] = load(w2_rows[2, 1], [P, PACK, H])
+        a1_raw[2] = load(a1_rows[2], [P, PACK, C])
+        mask(0)
+        da = {}
+        da[0] = derivative(0, dh[0])
+        prepare_w2(1)
+        dh[1] = first_product(1)
+        a3_raw[2] = load(a3_rows[2], [P, PACK, C])
+        dx = {}
+        dx[0] = second_product(0, da[0])
+        prepare_g(1, 1, planes)
+        mask(1)
+        da[1] = derivative(1, dh[1])
+        scatter(0, dx[0])
+        w2_raw[3, 0] = load(w2_rows[3, 0], [P, PACK, H])
+        w2_raw[3, 1] = load(w2_rows[3, 1], [P, PACK, H])
+        a1_raw[3] = load(a1_rows[3], [P, PACK, C])
+        a3_raw[3] = load(a3_rows[3], [P, PACK, C])
+        prepare_w2(2)
+        dh[2] = first_product(2)
+        dx[1] = second_product(1, da[1])
+        mask(2)
+        da[2] = derivative(2, dh[2])
+        prepare_w2(3)
+        dh[3] = first_product(3)
+        mask(3)
+        scatter(1, dx[1])
+        dx[2] = second_product(2, da[2])
+        da[3] = derivative(3, dh[3])
+        scatter(2, dx[2])
+        dx[3] = second_product(3, da[3])
+        scatter(3, dx[3])
+        nc.sync.dma_start(out, result[:])

@@ -16,7 +16,6 @@ U8 = mybir.dt.uint8
 E4M3X4 = mybir.dt.float8_e4m3fn_x4
 E5M2X4 = mybir.dt.float8_e5m2_x4
 MULT = mybir.AluOpType.mult
-RELU = mybir.ActivationFunctionType.Relu
 IS_GT = mybir.AluOpType.is_gt
 
 FLOPS = 2 * N * H * E * C + 2 * 2 * H * K * E * C
@@ -33,7 +32,7 @@ def tile_moe_bdx_glu_relu_kernel(tc, dyT, a1, a3, w2, w1, w3, gate, offs, out):
 
     with ExitStack() as ctx:
         held = ctx.enter_context(tc.tile_pool(name="held", bufs=1))
-        raw = ctx.enter_context(tc.tile_pool(name="raw", bufs=11))
+        raw = ctx.enter_context(tc.tile_pool(name="raw", bufs=10))
         gpool = ctx.enter_context(tc.tile_pool(name="gpool", bufs=2))
         work = ctx.enter_context(tc.tile_pool(name="work", bufs=2))
         codes = ctx.enter_context(tc.tile_pool(name="codes", bufs=6))
@@ -44,9 +43,9 @@ def tile_moe_bdx_glu_relu_kernel(tc, dyT, a1, a3, w2, w1, w3, gate, offs, out):
             nc.sync.dma_start(big[:], src)
             return big
 
-        def quantize(src, tag, dtype, bufs):
-            words = codes.tile([P, C], U32, tag=tag + "_w", bufs=bufs, align_bytes=64, name=tag + "_w")
-            scales = codes.tile([P, C], U8, tag=tag + "_s", bufs=bufs, align_bytes=64, name=tag + "_s")
+        def quantize(src, width, tag, dtype, bufs):
+            words = codes.tile([P, width], U32, tag=tag + "_w", bufs=bufs, align_bytes=64, name=tag + "_w")
+            scales = codes.tile([P, width], U8, tag=tag + "_s", bufs=bufs, align_bytes=64, name=tag + "_s")
             nc.vector.quantize_mx(out=words[:].bitcast(dtype), scales=scales[:], in_=src[:])
             return words, scales
 
@@ -58,56 +57,56 @@ def tile_moe_bdx_glu_relu_kernel(tc, dyT, a1, a3, w2, w1, w3, gate, offs, out):
             for t in range(PACK):
                 dy[c, t] = load(dy_rows[c, t], [P, T])
                 if c == 0 and t == 0:
-                    g0 = held.tile([P, PAIR], F32, name="g0")
-                    nc.sync.dma_start(g0[:], gate[0:P, 0:PAIR])
-                    gates[0] = g0
-        g1 = held.tile([P, PAIR], F32, name="g1")
-        nc.sync.dma_start(g1[:], gate[0:P, PAIR : 2 * PAIR])
-        gates[1] = g1
+                    for pair in range(2):
+                        gates[pair] = held.tile([P, PAIR], F32, name="gate%d" % pair)
+                    nc.sync.dma_start(gates[0][:, 0:C], gate[0:P, 0:C])
+                    nc.sync.dma_start(gates[0][:, C:PAIR], gate[0:P, C:PAIR])
         w2_raw = {}
+        a1_raw = {}
+        a3_raw = {}
         w2_raw[0, 0] = load(w2_rows[0, 0], [P, PACK, H])
+        nc.sync.dma_start(gates[1][:], gate[0:P, PAIR : 2 * PAIR])
         w2_raw[0, 1] = load(w2_rows[0, 1], [P, PACK, H])
-        w1_raw = load(w1.rearrange("e (p j) k -> p e j k", j=PACK), [P, E, PACK, K])
 
         result = held.tile([P, T], F32, name="result")
 
         g_q = {}
         w2_q = {}
 
-        def gather(pair, c, t, planes):
-            nc.vector.tensor_tensor(
-                planes[:, t, :],
-                dy[c, t][:].indirect(offsets[:, pair * PAIR // 16 : (pair + 1) * PAIR // 16]),
-                gates[pair][:],
-                MULT,
-            )
+        def gather(pair, c, t, planes, cuts=(0, PAIR)):
+            for lo, hi in zip(cuts, cuts[1:]):
+                nc.vector.tensor_tensor(
+                    planes[:, t, lo:hi],
+                    dy[c, t][:].indirect(offsets[:, (pair * PAIR + lo) // 16 : (pair * PAIR + hi) // 16]),
+                    gates[pair][:, lo:hi],
+                    MULT,
+                )
 
         def prepare_g(pair, c, planes):
-            for h in range(2):
-                e = 2 * pair + h
-                gb = work.tile([P, PACK * C], BF16, tag="gb", bufs=3, align_bytes=64, name="gb")
-                nc.scalar.copy(
-                    out=gb[:].rearrange("p (s i t) -> p s t i", i=4, t=PACK),
-                    in_=planes[:, :, h * C : (h + 1) * C].rearrange("p t (s i) -> p s t i", i=4),
-                )
-                g_q[e, c] = quantize(gb, "g", E5M2X4, 6)
+            gb = work.tile([P, PACK * PAIR], BF16, tag="gb", bufs=2, align_bytes=64, name="gb")
+            nc.scalar.copy(
+                out=gb[:].rearrange("p (s i t) -> p s t i", i=4, t=PACK),
+                in_=planes[:].rearrange("p t (s i) -> p s t i", i=4),
+            )
+            g_q[pair, c] = quantize(gb, PAIR, "g", E5M2X4, 3)
 
         def prepare_w2(e):
+            wb = work.tile([P, PASSES * PACK * H], BF16, tag="wb", bufs=2, align_bytes=64, name="wb")
             for c in range(PASSES):
-                wb = work.tile([P, PACK * H], BF16, tag="wb", bufs=2, align_bytes=64, name="wb")
                 nc.scalar.copy(
-                    out=wb[:].rearrange("p (t m j) -> p m j t", t=PACK, j=PACK),
+                    out=wb[:, c * PACK * H : (c + 1) * PACK * H].rearrange("p (t m j) -> p m j t", t=PACK, j=PACK),
                     in_=w2_raw[e, c][:].rearrange("p j (m t) -> p m j t", t=PACK),
                 )
-                w2_q[e, c] = quantize(wb, "w2", E4M3X4, 5)
+            w2_q[e] = quantize(wb, PASSES * H, "w2", E4M3X4, 3)
 
-        def prepare_w13(src, tag):
-            wb = work.tile([P, PACK * H], BF16, tag="wb", bufs=2, align_bytes=64, name="wb")
-            nc.scalar.copy(
-                out=wb[:].rearrange("p (e k j) -> p e k j", e=E, j=PACK),
-                in_=src[:].rearrange("p e j k -> p e k j"),
-            )
-            return quantize(wb, tag, E4M3X4, 1)
+        def prepare_w13():
+            wb = work.tile([P, PASSES * PACK * H], BF16, tag="wb", bufs=2, align_bytes=64, name="wb")
+            for n in range(2):
+                nc.scalar.copy(
+                    out=wb[:, n * PACK * H : (n + 1) * PACK * H].rearrange("p (e k j) -> p e k j", e=E, j=PACK),
+                    in_=w13_raw[n][:].rearrange("p e j k -> p e k j"),
+                )
+            return quantize(wb, 2 * E * K, "w13", E4M3X4, 1)
 
         def first_product(e):
             dh = work.tile([P, PACK, C], F32, tag="dh", bufs=2, align_bytes=64, name="dh")
@@ -116,22 +115,15 @@ def tile_moe_bdx_glu_relu_kernel(tc, dyT, a1, a3, w2, w1, w3, gate, offs, out):
                 for c in range(PASSES):
                     nc.tensor.matmul_mx(
                         out=bank[:],
-                        lhsT=w2_q[e, c][0][:, t * P : (t + 1) * P].bitcast(E4M3X4),
-                        lhsT_scale=w2_q[e, c][1][:, t * P : (t + 1) * P],
-                        rhs=g_q[e, c][0][:].bitcast(E5M2X4),
-                        rhs_scale=g_q[e, c][1][:],
+                        lhsT=w2_q[e][0][:, c * H + t * P : c * H + (t + 1) * P].bitcast(E4M3X4),
+                        lhsT_scale=w2_q[e][1][:, c * H + t * P : c * H + (t + 1) * P],
+                        rhs=g_q[e // 2, c][0][:, e % 2 * C : (e % 2 + 1) * C].bitcast(E5M2X4),
+                        rhs_scale=g_q[e // 2, c][1][:, e % 2 * C : (e % 2 + 1) * C],
                         start=(c == 0),
                         stop=(c == PASSES - 1),
                     )
-                nc.scalar.copy(out=dh[:, t, :], in_=bank[:])
+                nc.vector.scalar_tensor_tensor(dh[:, t, :], a1_raw[e][:, t, :], 0.0, bank[:], op0=IS_GT, op1=MULT)
             return dh
-
-        a1_raw = {}
-        a3_raw = {}
-
-        def mask(e):
-            nc.scalar.activation(a1_raw[e][:], a1_raw[e][:], RELU)
-            nc.vector.scalar_tensor_tensor(a3_raw[e][:], a1_raw[e][:], 0.0, a3_raw[e][:], op0=IS_GT, op1=MULT)
 
         def walk_in(x):
             return x[:].rearrange("p t (s i) -> p s t i", i=4)
@@ -145,15 +137,15 @@ def tile_moe_bdx_glu_relu_kernel(tc, dyT, a1, a3, w2, w1, w3, gate, offs, out):
             nc.vector.tensor_tensor(
                 d3[:].rearrange("p (s i t) -> p s t i", i=4, t=PACK), walk_in(a1_raw[e]), walk_in(dh), MULT
             )
-            return quantize(d1, "da", E5M2X4, 4), quantize(d3, "da", E5M2X4, 4)
+            return quantize(d1, C, "da", E5M2X4, 4), quantize(d3, C, "da", E5M2X4, 4)
 
         def second_product(e, da):
             bank = psum.tile([P, C], F32, tag="dx", bufs=2, name="dxbank")
-            for n, (wq, dq) in enumerate(zip((w1_q, w3_q), da)):
+            for n, dq in enumerate(da):
                 nc.tensor.matmul_mx(
                     out=bank[:],
-                    lhsT=wq[0][:, e * K : (e + 1) * K].bitcast(E4M3X4),
-                    lhsT_scale=wq[1][:, e * K : (e + 1) * K],
+                    lhsT=w13_q[0][:, (n * E + e) * K : (n * E + e + 1) * K].bitcast(E4M3X4),
+                    lhsT_scale=w13_q[1][:, (n * E + e) * K : (n * E + e + 1) * K],
                     rhs=dq[0][:].bitcast(E5M2X4),
                     rhs_scale=dq[1][:],
                     start=(n == 0),
@@ -169,63 +161,60 @@ def tile_moe_bdx_glu_relu_kernel(tc, dyT, a1, a3, w2, w1, w3, gate, offs, out):
         for c in range(PASSES):
             planes = gpool.tile([P, PACK, PAIR], F32, tag="planes", align_bytes=64, name="planes")
             for t in range(PACK):
-                gather(0, c, t, planes)
+                gather(0, c, t, planes, (0, C, PAIR) if c == 0 and t == 0 else (0, PAIR))
             prepare_g(0, c, planes)
         prepare_w2(0)
-        w1_q = prepare_w13(w1_raw, "w1")
 
+        w13_raw = {}
         planes = gpool.tile([P, PACK, PAIR], F32, tag="planes", align_bytes=64, name="planes")
         gather(1, 0, 0, planes)
-        w3_raw = load(w3.rearrange("e (p j) k -> p e j k", j=PACK), [P, E, PACK, K])
+        w13_raw[0] = load(w1.rearrange("e (p j) k -> p e j k", j=PACK), [P, E, PACK, K])
         gather(1, 0, 1, planes)
-        a1_raw[0] = load(a1_rows[0], [P, PACK, C])
+        w13_raw[1] = load(w3.rearrange("e (p j) k -> p e j k", j=PACK), [P, E, PACK, K])
         gather(1, 0, 2, planes)
-        a3_raw[0] = load(a3_rows[0], [P, PACK, C])
+        a1_raw[0] = load(a1_rows[0], [P, PACK, C])
         gather(1, 0, 3, planes)
-        w2_raw[1, 0] = load(w2_rows[1, 0], [P, PACK, H])
-        w3_q = prepare_w13(w3_raw, "w3")
+        a3_raw[0] = load(a3_rows[0], [P, PACK, C])
+        w13_q = prepare_w13()
         dh = {}
+        da = {}
+        dx = {}
         dh[0] = first_product(0)
         prepare_g(1, 0, planes)
         planes = gpool.tile([P, PACK, PAIR], F32, tag="planes", align_bytes=64, name="planes")
         gather(1, 1, 0, planes)
-        w2_raw[1, 1] = load(w2_rows[1, 1], [P, PACK, H])
+        w2_raw[1, 0] = load(w2_rows[1, 0], [P, PACK, H])
         gather(1, 1, 1, planes)
-        a1_raw[1] = load(a1_rows[1], [P, PACK, C])
+        w2_raw[1, 1] = load(w2_rows[1, 1], [P, PACK, H])
         gather(1, 1, 2, planes)
-        a3_raw[1] = load(a3_rows[1], [P, PACK, C])
+        a1_raw[1] = load(a1_rows[1], [P, PACK, C])
         gather(1, 1, 3, planes)
+        a3_raw[1] = load(a3_rows[1], [P, PACK, C])
         w2_raw[2, 0] = load(w2_rows[2, 0], [P, PACK, H])
         w2_raw[2, 1] = load(w2_rows[2, 1], [P, PACK, H])
-        a1_raw[2] = load(a1_rows[2], [P, PACK, C])
-        mask(0)
-        da = {}
-        da[0] = derivative(0, dh[0])
+        prepare_g(1, 1, planes)
         prepare_w2(1)
         dh[1] = first_product(1)
+        a1_raw[2] = load(a1_rows[2], [P, PACK, C])
         a3_raw[2] = load(a3_rows[2], [P, PACK, C])
-        dx = {}
-        dx[0] = second_product(0, da[0])
-        prepare_g(1, 1, planes)
-        mask(1)
-        da[1] = derivative(1, dh[1])
-        scatter(0, dx[0])
+        da[0] = derivative(0, dh[0])
         w2_raw[3, 0] = load(w2_rows[3, 0], [P, PACK, H])
         w2_raw[3, 1] = load(w2_rows[3, 1], [P, PACK, H])
-        a1_raw[3] = load(a1_rows[3], [P, PACK, C])
-        a3_raw[3] = load(a3_rows[3], [P, PACK, C])
+        dx[0] = second_product(0, da[0])
         prepare_w2(2)
         dh[2] = first_product(2)
-        dx[1] = second_product(1, da[1])
-        mask(2)
-        da[2] = derivative(2, dh[2])
+        da[1] = derivative(1, dh[1])
+        a1_raw[3] = load(a1_rows[3], [P, PACK, C])
+        a3_raw[3] = load(a3_rows[3], [P, PACK, C])
         prepare_w2(3)
         dh[3] = first_product(3)
-        mask(3)
+        scatter(0, dx[0])
+        dx[1] = second_product(1, da[1])
+        da[2] = derivative(2, dh[2])
         scatter(1, dx[1])
         dx[2] = second_product(2, da[2])
         da[3] = derivative(3, dh[3])
-        scatter(2, dx[2])
         dx[3] = second_product(3, da[3])
+        scatter(2, dx[2])
         scatter(3, dx[3])
         nc.sync.dma_start(out, result[:])

@@ -7,6 +7,9 @@ P = 128
 PACK = 4
 PASSES = N // (P * PACK)
 PAIR = 2 * C
+GQ = 3
+WQ = 2
+WR = 3
 
 F32 = mybir.dt.float32
 BF16 = mybir.dt.bfloat16
@@ -32,7 +35,8 @@ def tile_moe_bdx_glu_relu_kernel(tc, dyT, a1, a3, w2, w1, w3, gate, offs, out):
 
     with ExitStack() as ctx:
         held = ctx.enter_context(tc.tile_pool(name="held", bufs=1))
-        raw = ctx.enter_context(tc.tile_pool(name="raw", bufs=10))
+        raw = ctx.enter_context(tc.tile_pool(name="raw", bufs=8))
+        wraw = ctx.enter_context(tc.tile_pool(name="wraw", bufs=WR))
         gpool = ctx.enter_context(tc.tile_pool(name="gpool", bufs=2))
         work = ctx.enter_context(tc.tile_pool(name="work", bufs=2))
         codes = ctx.enter_context(tc.tile_pool(name="codes", bufs=6))
@@ -42,6 +46,11 @@ def tile_moe_bdx_glu_relu_kernel(tc, dyT, a1, a3, w2, w1, w3, gate, offs, out):
             big = raw.tile(shape, F32, tag="big", align_bytes=64, name="big")
             nc.sync.dma_start(big[:], src)
             return big
+
+        def load_w(src, shape):
+            mat = wraw.tile(shape, F32, tag="mat", align_bytes=64, name="mat")
+            nc.sync.dma_start(mat[:], src)
+            return mat
 
         def quantize(src, width, tag, dtype, bufs):
             words = codes.tile([P, width], U32, tag=tag + "_w", bufs=bufs, align_bytes=64, name=tag + "_w")
@@ -53,24 +62,31 @@ def tile_moe_bdx_glu_relu_kernel(tc, dyT, a1, a3, w2, w1, w3, gate, offs, out):
         nc.sync.dma_start(offsets[:], offs)
         dy = {}
         gates = {}
-        for c in range(PASSES):
-            for t in range(PACK):
-                dy[c, t] = load(dy_rows[c, t], [P, T])
-                if c == 0 and t == 0:
-                    for pair in range(2):
-                        gates[pair] = held.tile([P, PAIR], F32, name="gate%d" % pair)
-                    nc.sync.dma_start(gates[0][:, 0:C], gate[0:P, 0:C])
-                    nc.sync.dma_start(gates[0][:, C:PAIR], gate[0:P, C:PAIR])
         w2_raw = {}
+        w13_raw = {}
         a1_raw = {}
         a3_raw = {}
-        w2_raw[0, 0] = load(w2_rows[0, 0], [P, PACK, H])
-        nc.sync.dma_start(gates[1][:], gate[0:P, PAIR : 2 * PAIR])
-        w2_raw[0, 1] = load(w2_rows[0, 1], [P, PACK, H])
-
+        for pair in range(2):
+            gates[pair] = held.tile([P, PAIR], F32, name="gate%d" % pair)
+        dy[0, 0] = load(dy_rows[0, 0], [P, T])
+        nc.sync.dma_start(gates[0][:, 0:512], gate[0:P, 0:512])
+        nc.sync.dma_start(gates[0][:, 512:1024], gate[0:P, 512:1024])
+        dy[0, 1] = load(dy_rows[0, 1], [P, T])
+        dy[0, 2] = load(dy_rows[0, 2], [P, T])
+        dy[0, 3] = load(dy_rows[0, 3], [P, T])
+        dy[1, 0] = load(dy_rows[1, 0], [P, T])
+        dy[1, 1] = load(dy_rows[1, 1], [P, T])
+        dy[1, 2] = load(dy_rows[1, 2], [P, T])
+        w2_raw[0, 0] = load_w(w2_rows[0, 0], [P, PACK, H])
+        dy[1, 3] = load(dy_rows[1, 3], [P, T])
+        nc.sync.dma_start(gates[1][:, 0:1024], gate[0:P, 1024:2048])
+        w2_raw[0, 1] = load_w(w2_rows[0, 1], [P, PACK, H])
+        w13_raw[0] = load_w(w1.rearrange("e (p j) k -> p e j k", j=PACK), [P, E, PACK, K])
         result = held.tile([P, T], F32, name="result")
 
+        g_b = {}
         g_q = {}
+        w2_b = {}
         w2_q = {}
 
         def gather(pair, c, t, planes, cuts=(0, PAIR)):
@@ -88,25 +104,34 @@ def tile_moe_bdx_glu_relu_kernel(tc, dyT, a1, a3, w2, w1, w3, gate, offs, out):
                 out=gb[:].rearrange("p (s i t) -> p s t i", i=4, t=PACK),
                 in_=planes[:].rearrange("p t (s i) -> p s t i", i=4),
             )
-            g_q[pair, c] = quantize(gb, PAIR, "g", E5M2X4, 3)
+            g_b[pair, c] = gb
 
-        def prepare_w2(e):
-            wb = work.tile([P, PASSES * PACK * H], BF16, tag="wb", bufs=2, align_bytes=64, name="wb")
-            for c in range(PASSES):
-                nc.scalar.copy(
-                    out=wb[:, c * PACK * H : (c + 1) * PACK * H].rearrange("p (t m j) -> p m j t", t=PACK, j=PACK),
-                    in_=w2_raw[e, c][:].rearrange("p j (m t) -> p m j t", t=PACK),
-                )
-            w2_q[e] = quantize(wb, PASSES * H, "w2", E4M3X4, 3)
+        def quantize_g(pair, c):
+            g_q[pair, c] = quantize(g_b[pair, c], PAIR, "g", E5M2X4, GQ)
 
-        def prepare_w13():
-            wb = work.tile([P, PASSES * PACK * H], BF16, tag="wb", bufs=2, align_bytes=64, name="wb")
-            for n in range(2):
-                nc.scalar.copy(
-                    out=wb[:, n * PACK * H : (n + 1) * PACK * H].rearrange("p (e k j) -> p e k j", e=E, j=PACK),
-                    in_=w13_raw[n][:].rearrange("p e j k -> p e k j"),
-                )
-            return quantize(wb, 2 * E * K, "w13", E4M3X4, 1)
+        def round_w2(e, c):
+            if c == 0:
+                w2_b[e] = work.tile([P, PASSES * PACK * H], BF16, tag="wb", bufs=2, align_bytes=64, name="wb")
+            nc.scalar.copy(
+                out=w2_b[e][:, c * PACK * H : (c + 1) * PACK * H].rearrange("p (t m j) -> p m j t", t=PACK, j=PACK),
+                in_=w2_raw[e, c][:].rearrange("p j (m t) -> p m j t", t=PACK),
+            )
+
+        def quantize_w2(e):
+            w2_q[e] = quantize(w2_b[e], PASSES * H, "w2", E4M3X4, WQ)
+
+        w13_b = {}
+
+        def round_w13(n):
+            if n == 0:
+                w13_b[0] = work.tile([P, PASSES * PACK * H], BF16, tag="wb", bufs=2, align_bytes=64, name="wb")
+            nc.scalar.copy(
+                out=w13_b[0][:, n * PACK * H : (n + 1) * PACK * H].rearrange("p (e k j) -> p e k j", e=E, j=PACK),
+                in_=w13_raw[n][:].rearrange("p e j k -> p e k j"),
+            )
+
+        def quantize_w13():
+            return quantize(w13_b[0], 2 * E * K, "w13", E4M3X4, 1)
 
         def first_product(e):
             dh = work.tile([P, PACK, C], F32, tag="dh", bufs=2, align_bytes=64, name="dh")
@@ -129,8 +154,8 @@ def tile_moe_bdx_glu_relu_kernel(tc, dyT, a1, a3, w2, w1, w3, gate, offs, out):
             return x[:].rearrange("p t (s i) -> p s t i", i=4)
 
         def derivative(e, dh):
-            d1 = work.tile([P, PACK * C], BF16, tag="da", bufs=3, align_bytes=64, name="d1")
-            d3 = work.tile([P, PACK * C], BF16, tag="da", bufs=3, align_bytes=64, name="d3")
+            d1 = work.tile([P, PACK * C], BF16, tag="da", bufs=2, align_bytes=64, name="d1")
+            d3 = work.tile([P, PACK * C], BF16, tag="da", bufs=2, align_bytes=64, name="d3")
             nc.vector.tensor_tensor(
                 d1[:].rearrange("p (s i t) -> p s t i", i=4, t=PACK), walk_in(a3_raw[e]), walk_in(dh), MULT
             )
@@ -158,61 +183,79 @@ def tile_moe_bdx_glu_relu_kernel(tc, dyT, a1, a3, w2, w1, w3, gate, offs, out):
         def scatter(e, dx):
             nc.vector.tensor_copy(result[:].indirect(offsets[:, e * C // 16 : (e + 1) * C // 16]), dx[:])
 
-        for c in range(PASSES):
-            planes = gpool.tile([P, PACK, PAIR], F32, tag="planes", align_bytes=64, name="planes")
-            for t in range(PACK):
-                gather(0, c, t, planes, (0, C, PAIR) if c == 0 and t == 0 else (0, PAIR))
-            prepare_g(0, c, planes)
-        prepare_w2(0)
-
-        w13_raw = {}
-        planes = gpool.tile([P, PACK, PAIR], F32, tag="planes", align_bytes=64, name="planes")
-        gather(1, 0, 0, planes)
-        w13_raw[0] = load(w1.rearrange("e (p j) k -> p e j k", j=PACK), [P, E, PACK, K])
-        gather(1, 0, 1, planes)
-        w13_raw[1] = load(w3.rearrange("e (p j) k -> p e j k", j=PACK), [P, E, PACK, K])
-        gather(1, 0, 2, planes)
-        a1_raw[0] = load(a1_rows[0], [P, PACK, C])
-        gather(1, 0, 3, planes)
-        a3_raw[0] = load(a3_rows[0], [P, PACK, C])
-        w13_q = prepare_w13()
         dh = {}
         da = {}
         dx = {}
+        planes = gpool.tile([P, PACK, PAIR], F32, tag="planes", align_bytes=64, name="planes")
+        gather(0, 0, 0, planes, (0, C, PAIR))
+        gather(0, 0, 1, planes)
+        gather(0, 0, 2, planes)
+        gather(0, 0, 3, planes)
+        prepare_g(0, 0, planes)
+        round_w2(0, 0)
+        w13_raw[1] = load_w(w3.rearrange("e (p j) k -> p e j k", j=PACK), [P, E, PACK, K])
+        planes = gpool.tile([P, PACK, PAIR], F32, tag="planes", align_bytes=64, name="planes")
+        gather(0, 1, 0, planes)
+        gather(0, 1, 1, planes)
+        gather(0, 1, 2, planes)
+        gather(0, 1, 3, planes)
+        prepare_g(0, 1, planes)
+        round_w2(0, 1)
+        w2_raw[1, 0] = load_w(w2_rows[1, 0], [P, PACK, H])
+        round_w13(0)
+        w2_raw[1, 1] = load_w(w2_rows[1, 1], [P, PACK, H])
+        round_w13(1)
+        planes = gpool.tile([P, PACK, PAIR], F32, tag="planes", align_bytes=64, name="planes")
+        gather(1, 0, 0, planes)
+        a1_raw[0] = load(a1_rows[0], [P, PACK, C])
+        gather(1, 0, 1, planes)
+        a3_raw[0] = load(a3_rows[0], [P, PACK, C])
+        gather(1, 0, 2, planes)
+        a1_raw[1] = load(a1_rows[1], [P, PACK, C])
+        gather(1, 0, 3, planes)
+        a3_raw[1] = load(a3_rows[1], [P, PACK, C])
+        round_w2(1, 0)
+        w2_raw[2, 0] = load_w(w2_rows[2, 0], [P, PACK, H])
+        round_w2(1, 1)
+        w2_raw[2, 1] = load_w(w2_rows[2, 1], [P, PACK, H])
+        quantize_g(0, 0)
+        quantize_g(0, 1)
+        quantize_w2(0)
         dh[0] = first_product(0)
         prepare_g(1, 0, planes)
         planes = gpool.tile([P, PACK, PAIR], F32, tag="planes", align_bytes=64, name="planes")
         gather(1, 1, 0, planes)
-        w2_raw[1, 0] = load(w2_rows[1, 0], [P, PACK, H])
         gather(1, 1, 1, planes)
-        w2_raw[1, 1] = load(w2_rows[1, 1], [P, PACK, H])
         gather(1, 1, 2, planes)
-        a1_raw[1] = load(a1_rows[1], [P, PACK, C])
         gather(1, 1, 3, planes)
-        a3_raw[1] = load(a3_rows[1], [P, PACK, C])
-        w2_raw[2, 0] = load(w2_rows[2, 0], [P, PACK, H])
-        w2_raw[2, 1] = load(w2_rows[2, 1], [P, PACK, H])
         prepare_g(1, 1, planes)
-        prepare_w2(1)
+        w2_raw[3, 0] = load_w(w2_rows[3, 0], [P, PACK, H])
+        da[0] = derivative(0, dh[0])
+        w13_q = quantize_w13()
+        quantize_w2(1)
         dh[1] = first_product(1)
+        dx[0] = second_product(0, da[0])
+        da[1] = derivative(1, dh[1])
+        round_w2(2, 0)
+        w2_raw[3, 1] = load_w(w2_rows[3, 1], [P, PACK, H])
+        round_w2(2, 1)
         a1_raw[2] = load(a1_rows[2], [P, PACK, C])
         a3_raw[2] = load(a3_rows[2], [P, PACK, C])
-        da[0] = derivative(0, dh[0])
-        w2_raw[3, 0] = load(w2_rows[3, 0], [P, PACK, H])
-        w2_raw[3, 1] = load(w2_rows[3, 1], [P, PACK, H])
-        dx[0] = second_product(0, da[0])
-        prepare_w2(2)
+        dx[1] = second_product(1, da[1])
+        scatter(0, dx[0])
+        quantize_g(1, 0)
+        quantize_g(1, 1)
+        round_w2(3, 0)
+        round_w2(3, 1)
+        quantize_w2(2)
         dh[2] = first_product(2)
-        da[1] = derivative(1, dh[1])
         a1_raw[3] = load(a1_rows[3], [P, PACK, C])
         a3_raw[3] = load(a3_rows[3], [P, PACK, C])
-        prepare_w2(3)
-        dh[3] = first_product(3)
-        scatter(0, dx[0])
-        dx[1] = second_product(1, da[1])
         da[2] = derivative(2, dh[2])
-        scatter(1, dx[1])
+        quantize_w2(3)
+        dh[3] = first_product(3)
         dx[2] = second_product(2, da[2])
+        scatter(1, dx[1])
         da[3] = derivative(3, dh[3])
         dx[3] = second_product(3, da[3])
         scatter(2, dx[2])

@@ -151,16 +151,16 @@ def tile_moe_bdx_glu_relu_kernel(tc, dyT, a1, a3, w2, w1, w3, gate, offs, out):
             return dh
 
         def walk_in(x):
-            return x[:].rearrange("p t (s i) -> p s t i", i=4)
+            return x[:].rearrange("p t (s i) -> p s t i", i=2)
 
         def derivative(e, dh):
             d1 = work.tile([P, PACK * C], BF16, tag="da", bufs=2, align_bytes=64, name="d1")
             d3 = work.tile([P, PACK * C], BF16, tag="da", bufs=2, align_bytes=64, name="d3")
             nc.vector.tensor_tensor(
-                d1[:].rearrange("p (s i t) -> p s t i", i=4, t=PACK), walk_in(a3_raw[e]), walk_in(dh), MULT
+                d1[:].rearrange("p (s i t) -> p s t i", i=2, t=PACK), walk_in(a3_raw[e]), walk_in(dh), MULT
             )
             nc.vector.tensor_tensor(
-                d3[:].rearrange("p (s i t) -> p s t i", i=4, t=PACK), walk_in(a1_raw[e]), walk_in(dh), MULT
+                d3[:].rearrange("p (s i t) -> p s t i", i=2, t=PACK), walk_in(a1_raw[e]), walk_in(dh), MULT
             )
             return quantize(d1, C, "da", E5M2X4, 4), quantize(d3, C, "da", E5M2X4, 4)
 

from contextlib import ExitStack

import concourse.mybir as mybir

E, C, T, K, H, N = 4, 512, 2048, 128, 512, 1024
P = 128
PACK = 4
PASSES = N // (P * PACK)
PAIR = 2 * C
GQ = 3
WQ = 2
WR = 3

F32 = mybir.dt.float32
BF16 = mybir.dt.bfloat16
U32 = mybir.dt.uint32
U16 = mybir.dt.uint16
U8 = mybir.dt.uint8
E4M3X4 = mybir.dt.float8_e4m3fn_x4
E5M2X4 = mybir.dt.float8_e5m2_x4
MULT = mybir.AluOpType.mult
IS_GT = mybir.AluOpType.is_gt

FLOPS = 2 * N * H * E * C + 2 * 2 * H * K * E * C
BYTES = 4 * (N * T + 2 * H * E * C + E * N * H + 2 * E * H * K + E * C + K * T) + 2 * P * (E * C // 16)


def tile_moe_bdx_glu_relu_kernel(tc, dyT, a1, a3, w2, w1, w3, gate, offs, out):
    nc = tc.nc

    dy_rows = dyT.rearrange("(c p t) w -> c t p w", c=PASSES, t=PACK)
    w2_rows = w2.rearrange("e (c p j) i -> e c p j i", c=PASSES, j=PACK)
    a1_rows = a1.rearrange("(p t) (e s) -> e p t s", t=PACK, e=E)
    a3_rows = a3.rearrange("(p t) (e s) -> e p t s", t=PACK, e=E)

    with ExitStack() as ctx:
        held = ctx.enter_context(tc.tile_pool(name="held", bufs=1))
        raw = ctx.enter_context(tc.tile_pool(name="raw", bufs=8))
        wraw = ctx.enter_context(tc.tile_pool(name="wraw", bufs=WR))
        gpool = ctx.enter_context(tc.tile_pool(name="gpool", bufs=2))
        work = ctx.enter_context(tc.tile_pool(name="work", bufs=2))
        codes = ctx.enter_context(tc.tile_pool(name="codes", bufs=6))
        psum = ctx.enter_context(tc.psum_pool(name="psum", bufs=1))

        def load(src, shape):
            big = raw.tile(shape, F32, tag="big", align_bytes=64, name="big")
            nc.sync.dma_start(big[:], src)
            return big

        def load_w(src, shape):
            mat = wraw.tile(shape, F32, tag="mat", align_bytes=64, name="mat")
            nc.sync.dma_start(mat[:], src)
            return mat

        def quantize(src, width, tag, dtype, bufs):
            words = codes.tile([P, width], U32, tag=tag + "_w", bufs=bufs, align_bytes=64, name=tag + "_w")
            scales = codes.tile([P, width], U8, tag=tag + "_s", bufs=bufs, align_bytes=64, name=tag + "_s")
            nc.vector.quantize_mx(out=words[:].bitcast(dtype), scales=scales[:], in_=src[:])
            return words, scales

        offsets = held.tile([P, E * C // 16], U16, name="offsets")
        nc.sync.dma_start(offsets[:], offs)
        dy = {}
        gates = {}
        w2_raw = {}
        w13_raw = {}
        a1_raw = {}
        a3_raw = {}
        for pair in range(2):
            gates[pair] = held.tile([P, PAIR], F32, name="gate%d" % pair)
        dy[0, 0] = load(dy_rows[0, 0], [P, T])
        nc.sync.dma_start(gates[0][:, 0:512], gate[0:P, 0:512])
        nc.sync.dma_start(gates[0][:, 512:1024], gate[0:P, 512:1024])
        dy[0, 1] = load(dy_rows[0, 1], [P, T])
        dy[0, 2] = load(dy_rows[0, 2], [P, T])
        dy[0, 3] = load(dy_rows[0, 3], [P, T])
        dy[1, 0] = load(dy_rows[1, 0], [P, T])
        dy[1, 1] = load(dy_rows[1, 1], [P, T])
        dy[1, 2] = load(dy_rows[1, 2], [P, T])
        w2_raw[0, 0] = load_w(w2_rows[0, 0], [P, PACK, H])
        dy[1, 3] = load(dy_rows[1, 3], [P, T])
        nc.sync.dma_start(gates[1][:, 0:1024], gate[0:P, 1024:2048])
        w2_raw[0, 1] = load_w(w2_rows[0, 1], [P, PACK, H])
        w13_raw[0] = load_w(w1.rearrange("e (p j) k -> p e j k", j=PACK), [P, E, PACK, K])
        result = held.tile([P, T], F32, name="result")

        g_b = {}
        g_q = {}
        w2_b = {}
        w2_q = {}

        def gather(pair, c, t, planes, cuts=(0, PAIR)):
            for lo, hi in zip(cuts, cuts[1:]):
                nc.vector.tensor_tensor(
                    planes[:, t, lo:hi],
                    dy[c, t][:].indirect(offsets[:, (pair * PAIR + lo) // 16 : (pair * PAIR + hi) // 16]),
                    gates[pair][:, lo:hi],
                    MULT,
                )

        def prepare_g(pair, c, planes):
            gb = work.tile([P, PACK * PAIR], BF16, tag="gb", bufs=2, align_bytes=64, name="gb")
            nc.scalar.copy(
                out=gb[:].rearrange("p (s i t) -> p s t i", i=4, t=PACK),
                in_=planes[:].rearrange("p t (s i) -> p s t i", i=4),
            )
            g_b[pair, c] = gb

        def quantize_g(pair, c):
            g_q[pair, c] = quantize(g_b[pair, c], PAIR, "g", E5M2X4, GQ)

        def round_w2(e, c):
            if c == 0:
                w2_b[e] = work.tile([P, PASSES * PACK * H], BF16, tag="wb", bufs=2, align_bytes=64, name="wb")
            nc.scalar.copy(
                out=w2_b[e][:, c * PACK * H : (c + 1) * PACK * H].rearrange("p (t m j) -> p m j t", t=PACK, j=PACK),
                in_=w2_raw[e, c][:].rearrange("p j (m t) -> p m j t", t=PACK),
            )

        def quantize_w2(e):
            w2_q[e] = quantize(w2_b[e], PASSES * H, "w2", E4M3X4, WQ)

        w13_b = {}

        def round_w13(n):
            if n == 0:
                w13_b[0] = work.tile([P, PASSES * PACK * H], BF16, tag="wb", bufs=2, align_bytes=64, name="wb")
            nc.scalar.copy(
                out=w13_b[0][:, n * PACK * H : (n + 1) * PACK * H].rearrange("p (e k j) -> p e k j", e=E, j=PACK),
                in_=w13_raw[n][:].rearrange("p e j k -> p e k j"),
            )

        def quantize_w13():
            return quantize(w13_b[0], 2 * E * K, "w13", E4M3X4, 1)

        def first_product(e):
            dh = work.tile([P, PACK, C], F32, tag="dh", bufs=2, align_bytes=64, name="dh")
            for t in range(PACK):
                bank = psum.tile([P, C], F32, tag="bank", bufs=6, name="bank")
                for c in range(PASSES):
                    nc.tensor.matmul_mx(
                        out=bank[:],
                        lhsT=w2_q[e][0][:, c * H + t * P : c * H + (t + 1) * P].bitcast(E4M3X4),
                        lhsT_scale=w2_q[e][1][:, c * H + t * P : c * H + (t + 1) * P],
                        rhs=g_q[e // 2, c][0][:, e % 2 * C : (e % 2 + 1) * C].bitcast(E5M2X4),
                        rhs_scale=g_q[e // 2, c][1][:, e % 2 * C : (e % 2 + 1) * C],
                        start=(c == 0),
                        stop=(c == PASSES - 1),
                    )
                nc.vector.scalar_tensor_tensor(dh[:, t, :], a1_raw[e][:, t, :], 0.0, bank[:], op0=IS_GT, op1=MULT)
            return dh

        def walk_in(x):
            return x[:].rearrange("p t (s i) -> p s t i", i=2)

        def derivative(e, dh):
            d1 = work.tile([P, PACK * C], BF16, tag="da", bufs=2, align_bytes=64, name="d1")
            d3 = work.tile([P, PACK * C], BF16, tag="da", bufs=2, align_bytes=64, name="d3")
            nc.vector.tensor_tensor(
                d1[:].rearrange("p (s i t) -> p s t i", i=2, t=PACK), walk_in(a3_raw[e]), walk_in(dh), MULT
            )
            nc.vector.tensor_tensor(
                d3[:].rearrange("p (s i t) -> p s t i", i=2, t=PACK), walk_in(a1_raw[e]), walk_in(dh), MULT
            )
            return quantize(d1, C, "da", E5M2X4, 4), quantize(d3, C, "da", E5M2X4, 4)

        def second_product(e, da):
            bank = psum.tile([P, C], F32, tag="dx", bufs=2, name="dxbank")
            for n, dq in enumerate(da):
                nc.tensor.matmul_mx(
                    out=bank[:],
                    lhsT=w13_q[0][:, (n * E + e) * K : (n * E + e + 1) * K].bitcast(E4M3X4),
                    lhsT_scale=w13_q[1][:, (n * E + e) * K : (n * E + e + 1) * K],
                    rhs=dq[0][:].bitcast(E5M2X4),
                    rhs_scale=dq[1][:],
                    start=(n == 0),
                    stop=(n == 1),
                )
            dx = work.tile([P, C], F32, tag="dx", bufs=2, align_bytes=64, name="dx")
            nc.scalar.copy(out=dx[:], in_=bank[:])
            return dx

        def scatter(e, dx):
            nc.vector.tensor_copy(result[:].indirect(offsets[:, e * C // 16 : (e + 1) * C // 16]), dx[:])

        dh = {}
        da = {}
        dx = {}
        planes = gpool.tile([P, PACK, PAIR], F32, tag="planes", align_bytes=64, name="planes")
        gather(0, 0, 0, planes, (0, C, PAIR))
        gather(0, 0, 1, planes)
        gather(0, 0, 2, planes)
        gather(0, 0, 3, planes)
        prepare_g(0, 0, planes)
        round_w2(0, 0)
        w13_raw[1] = load_w(w3.rearrange("e (p j) k -> p e j k", j=PACK), [P, E, PACK, K])
        planes = gpool.tile([P, PACK, PAIR], F32, tag="planes", align_bytes=64, name="planes")
        gather(0, 1, 0, planes)
        gather(0, 1, 1, planes)
        gather(0, 1, 2, planes)
        gather(0, 1, 3, planes)
        prepare_g(0, 1, planes)
        round_w2(0, 1)
        w2_raw[1, 0] = load_w(w2_rows[1, 0], [P, PACK, H])
        round_w13(0)
        w2_raw[1, 1] = load_w(w2_rows[1, 1], [P, PACK, H])
        round_w13(1)
        planes = gpool.tile([P, PACK, PAIR], F32, tag="planes", align_bytes=64, name="planes")
        gather(1, 0, 0, planes)
        a1_raw[0] = load(a1_rows[0], [P, PACK, C])
        gather(1, 0, 1, planes)
        a3_raw[0] = load(a3_rows[0], [P, PACK, C])
        gather(1, 0, 2, planes)
        a1_raw[1] = load(a1_rows[1], [P, PACK, C])
        gather(1, 0, 3, planes)
        a3_raw[1] = load(a3_rows[1], [P, PACK, C])
        round_w2(1, 0)
        w2_raw[2, 0] = load_w(w2_rows[2, 0], [P, PACK, H])
        round_w2(1, 1)
        w2_raw[2, 1] = load_w(w2_rows[2, 1], [P, PACK, H])
        quantize_g(0, 0)
        quantize_g(0, 1)
        quantize_w2(0)
        dh[0] = first_product(0)
        prepare_g(1, 0, planes)
        planes = gpool.tile([P, PACK, PAIR], F32, tag="planes", align_bytes=64, name="planes")
        gather(1, 1, 0, planes)
        gather(1, 1, 1, planes)
        gather(1, 1, 2, planes)
        gather(1, 1, 3, planes)
        prepare_g(1, 1, planes)
        w2_raw[3, 0] = load_w(w2_rows[3, 0], [P, PACK, H])
        da[0] = derivative(0, dh[0])
        w13_q = quantize_w13()
        quantize_w2(1)
        dh[1] = first_product(1)
        dx[0] = second_product(0, da[0])
        da[1] = derivative(1, dh[1])
        round_w2(2, 0)
        w2_raw[3, 1] = load_w(w2_rows[3, 1], [P, PACK, H])
        round_w2(2, 1)
        a1_raw[2] = load(a1_rows[2], [P, PACK, C])
        a3_raw[2] = load(a3_rows[2], [P, PACK, C])
        dx[1] = second_product(1, da[1])
        scatter(0, dx[0])
        quantize_g(1, 0)
        quantize_g(1, 1)
        round_w2(3, 0)
        round_w2(3, 1)
        quantize_w2(2)
        dh[2] = first_product(2)
        a1_raw[3] = load(a1_rows[3], [P, PACK, C])
        a3_raw[3] = load(a3_rows[3], [P, PACK, C])
        da[2] = derivative(2, dh[2])
        quantize_w2(3)
        dh[3] = first_product(3)
        dx[2] = second_product(2, da[2])
        scatter(1, dx[1])
        da[3] = derivative(3, dh[3])
        dx[3] = second_product(3, da[3])
        scatter(2, dx[2])
        scatter(3, dx[3])
        nc.sync.dma_start(out, result[:])
